import numpy as np
import ml_dtypes


def mxq(x, axis, fmt="e4m3"):
    dtype, down = {"e4m3": (ml_dtypes.float8_e4m3fn, 7), "e5m2": (ml_dtypes.float8_e5m2, 14)}[fmt]
    v = np.moveaxis(np.asarray(x, np.float32).astype(ml_dtypes.bfloat16).astype(np.float64), axis, -1)
    blocks = v.reshape(v.shape[:-1] + (-1, 32))
    amax = np.abs(blocks).max(-1, keepdims=True)
    byte = np.maximum(np.where(amax > 0, np.frexp(amax)[1] - 1 + 127, 0) - down, 1)
    scale = np.exp2(byte - 127.0)
    codes = (blocks / scale).astype(np.float32).astype(dtype).astype(np.float64)
    return np.moveaxis((codes * scale).reshape(v.shape), -1, axis)


WIDE = False


def mx_kscale(k):
    if not WIDE:
        return np.ones(k)
    levels = np.array([10, -10, 5, -5, 0])
    if k % 512:
        return np.exp2(np.random.permutation(np.resize(levels, k // 32))).repeat(32)
    a = np.empty((k // 512, 16))
    for p in range(k // 512):
        a[p, :8] = np.random.permutation(np.resize(levels, 8))
        for g in range(8):
            far = levels[np.abs(levels - a[p, g]) >= 10]
            a[p, g + 8] = far[np.random.randint(len(far))]
    return np.exp2(a.ravel()).repeat(32)


BF16 = ml_dtypes.bfloat16


def bf(x):
    return np.asarray(x, np.float32).astype(BF16)


def f64(x):
    return np.asarray(x).astype(np.float64)


E2M1 = np.array([0.0, 0.5, 1.0, 1.5, 2.0, 3.0, 4.0, 6.0, -0.0, -0.5, -1.0, -1.5, -2.0, -3.0, -4.0, -6.0])


def pack_weight(w, fmt):
    k, n = w.shape
    w = f64(bf(w)).reshape(k // 32, 32, n)
    amax = np.abs(w).max(1)
    if fmt == "e4m3":
        byte = np.frexp(amax)[1] - 1 + 127 - 7
    else:
        mant, ex = np.frexp(amax / 6.0)
        byte = np.where(mant > 0.5, ex, ex - 1) + 127
    byte = np.clip(np.where(amax > 0, byte, 1), 1, 254)
    scaled = (w * np.exp2(127.0 - byte)[:, None, :]).reshape(k, n).astype(np.float32)
    by_word = np.ascontiguousarray(scaled.reshape(k // 512, 128, 4, n).transpose(0, 1, 3, 2))
    if fmt == "e4m3":
        words = by_word.astype(ml_dtypes.float8_e4m3fn).view(np.uint8)
    else:
        c = by_word.astype(ml_dtypes.float4_e2m1fn).view(np.uint8) & 0xF
        words = c[..., 0::2] | (c[..., 1::2] << 4)
    return np.ascontiguousarray(words), np.ascontiguousarray(byte.astype(np.uint8).reshape(k // 512, 16, n))


def unpack_weight(words, scales, fmt):
    g, p, n, _ = words.shape
    if fmt == "e4m3":
        vals = np.ascontiguousarray(words).view(ml_dtypes.float8_e4m3fn).astype(np.float64)
    else:
        nib = np.empty((g, p, n, 4), np.uint8)
        nib[..., 0::2] = words & 0xF
        nib[..., 1::2] = words >> 4
        vals = E2M1[nib]
    vals = vals * np.repeat(np.exp2(scales.astype(np.float64) - 127.0), 8, axis=1)[..., None]
    return vals.transpose(0, 1, 3, 2).reshape(g * 512, n)
def pack4(w):
    words, scales = pack_weight(w, "e2m1")
    return words.reshape(words.shape[0], 128, -1), scales


def unpack4(words, scales):
    return unpack_weight(words.reshape(words.shape[0], 128, -1, 2), scales, "e2m1")


T, KH, KL, N = 2048, 512, 1024, 1024

SOFT2 = 0.125


def setup_inputs():
    s = mx_kscale(KH)
    v = mx_kscale(KL)
    gram = np.random.uniform(-1.0, 1.0, (T, KH + KL))
    mass = (1.0 + 0.1 * np.random.standard_normal(KH + KL)) * np.concatenate([s, v])
    heavy = np.random.standard_normal((KH, N)) / np.sqrt(KH) / s[:, None]
    light = np.random.standard_normal((KL, N)) / np.sqrt(KL) / v[:, None]
    light_words, light_scales = pack4(light)
    return {"gram": bf(gram),
            "mass": bf(mass),
            "heavy": bf(heavy),
            "light_words": light_words,
            "light_scales": light_scales,
            "background": bf(0.3 * np.random.standard_normal(N))}


def reference(gram, mass, heavy, light_words, light_scales, background):
    inv = (2.0 + SOFT2 - 2.0 * f64(gram)) ** -0.5
    a = inv * f64(mass)[None, :]
    ah = mxq(a[:, :KH], 1, "e4m3")
    al = mxq(a[:, KH:], 1, "e4m3")
    ch = mxq(f64(heavy), 0, "e4m3")
    cl = unpack4(light_words, light_scales)
    phi = (ah @ ch) + (al @ cl)
    return phi + f64(background)[None, :]

@@ -1,0 +1,330 @@
+from contextlib import ExitStack
+
+import concourse.mybir as mybir
+from concourse.masks import make_identity
+
+T, KH, KL, N = 2048, 512, 1024, 1024
+K = KH + KL
+FLOPS = 2 * T * K * N
+
+F32 = mybir.dt.float32
+BF16 = mybir.dt.bfloat16
+I32 = mybir.dt.int32
+U32 = mybir.dt.uint32
+U8 = mybir.dt.uint8
+FP8X4 = mybir.dt.float8_e4m3fn_x4
+FP4X4 = mybir.dt.float4_e2m1fn_x4
+ACT = mybir.ActivationFunctionType
+ALU = mybir.AluOpType
+
+SOFT2 = 0.125
+P = 128
+PACK = 4
+GROUP = 512
+GROUPS = K // GROUP
+SUBS = [1, 2, 2, 2, 2, 2, 2, 2, 1]
+STARTS = [P * sum(SUBS[:c]) for c in range(len(SUBS))]
+CHUNKS = len(SUBS)
+HALF = 512
+LOADS = ["g0", "s", "b", "g1", "L", "h0", "h1"] + ["g%d" % c for c in range(2, CHUNKS)]
+H_ENG = "vs"
+G_ORDER = (0, 1, 2)
+Q_ORDER = (1, 2, 0)
+HALVES = N // HALF
+
+
+def tile_shell_nbody_potential_s1_kernel(tc, gram, mass, heavy, light_words, light_scales, background, out):
+    nc = tc.nc
+    gram_rows = [gram[a : a + P * s, :].rearrange("(p s) k -> p s k", s=s) for a, s in zip(STARTS, SUBS)]
+    out_rows = [out[a : a + P * s, :].rearrange("(p s) n -> p s n", s=s) for a, s in zip(STARTS, SUBS)]
+
+    def pieces(c, g):
+        sub = SUBS[c]
+        if c < 3:
+            return [(0, sub, "v")]
+        if g == 0:
+            return [(0, sub, "g")]
+        if g == 1 and sub == 2:
+            return [(0, 1, "s"), (1, 2, "v")]
+        return [(0, sub, "v")]
+
+    with ExitStack() as ctx:
+        keep = ctx.enter_context(tc.tile_pool(name="keep", bufs=1))
+        work = ctx.enter_context(tc.tile_pool(name="work", bufs=3))
+        turn = ctx.enter_context(tc.psum_pool(name="turn", bufs=3))
+        fixed = ctx.enter_context(tc.psum_pool(name="fixed", bufs=1))
+        sums = ctx.enter_context(tc.psum_pool(name="sums", bufs=4))
+        ctx.enter_context(tc.manual_schedule())
+
+        grams = []
+        for c in range(CHUNKS):
+            g_sb = keep.tile([P, SUBS[c], K], BF16, name="gram%d" % c, align_bytes=64)
+            grams.append(g_sb)
+        mass_raw = keep.tile([P, GROUPS * PACK], BF16, name="mass_raw", align_bytes=64)
+        bg_rows = keep.tile([P, P], BF16, name="bg_rows", align_bytes=64)
+        mass_sq = keep.tile([P, P], BF16, name="mass_sq", align_bytes=64)
+        l_words = keep.tile([P, 2, 2 * N], U8, name="l_words", align_bytes=64)
+        l_scales = keep.tile([P, 2, N], U8, name="l_scales", align_bytes=64)
+        h_raw = keep.tile([P, PACK, N], BF16, name="h_raw", align_bytes=64)
+        ident32 = keep.tile([P, P], F32, name="ident32", align_bytes=64)
+        ident16 = keep.tile([P, P], BF16, name="ident16", align_bytes=64)
+        soft = keep.tile([P, 1], F32, name="soft", align_bytes=64)
+        warm = keep.tile([P, 1], F32, name="warm", align_bytes=64)
+
+        make_identity(nc, ident32[:])
+        nc.vector.memset(soft[:], 2.0 + SOFT2)
+        nc.vector.memset(bg_rows[:], 0.0)
+        nc.vector.memset(l_scales[:].rearrange("p g n -> p (g n)").bitcast(I32), 0)
+        nc.vector.memset(mass_sq[:], 0.0)
+
+        nc.scalar.dma_start(out=mass_raw[:].rearrange("p (g t) -> p g t", t=PACK), in_=mass.rearrange("(g p t) -> p g t", p=P, t=PACK))
+        heavy_rows = heavy.rearrange("(p j) n -> p j n", j=PACK)
+
+        def load(what):
+            if what[0] == "g":
+                c = int(what[1:])
+                nc.sync.dma_start(out=grams[c][:], in_=gram_rows[c])
+            elif what == "L":
+                nc.sync.dma_start(out=l_words[:].bitcast(I32), in_=light_words.rearrange("g p b -> p g b").bitcast(I32))
+            elif what == "b":
+                nc.sync.dma_start(out=bg_rows[0:8, :], in_=background.rearrange("(j c) -> j c", c=P))
+            elif what == "s":
+                for q in range(4):
+                    nc.sync.dma_start(
+                        out=l_scales[32 * q : 32 * q + 4, :, :].bitcast(I32),
+                        in_=light_scales[:, 4 * q : 4 * q + 4, :].rearrange("g q n -> q g n").bitcast(I32),
+                    )
+            else:
+                h = int(what[1:])
+                nc.sync.dma_start(out=h_raw[:, :, h * HALF : (h + 1) * HALF], in_=heavy_rows[:, :, h * HALF : (h + 1) * HALF])
+
+        for what in LOADS:
+            load(what)
+        nc.scalar.activation(out=warm[:], in_=soft[:], func=ACT.Abs_reciprocal_sqrt)
+
+        nc.vector.tensor_copy(out=ident16[:], in_=ident32[:])
+        nc.vector.tensor_copy(out=mass_sq[:, 0 : GROUPS * PACK], in_=mass_raw[:])
+        mass32 = keep.tile([P, GROUPS * PACK], F32, name="mass32", align_bytes=64)
+        nc.vector.tensor_copy(out=mass32[:], in_=mass_raw[:])
+
+        h_group = keep.tile([P, N, PACK], BF16, name="h_group", align_bytes=64)
+        h_codes = keep.tile([P, N], U32, name="h_codes", align_bytes=64)
+        h_scales = keep.tile([P, N], U8, name="h_scales", align_bytes=64)
+        mass_ps = fixed.tile([P, P], BF16, name="mass_ps")
+        bg = keep.tile([P, N], BF16, name="bg", align_bytes=64)
+
+        def transposes(c, g):
+            sub = SUBS[c]
+            bank = turn.tile([P, 2 * sub * P], F32, name="bank", tag="turn")
+            words = grams[c][:].rearrange("p s k -> p (s k)").bitcast(F32)
+            for u in range(2):
+                for s in range(sub):
+                    lo = s * (K // 2) + g * (GROUP // 2)
+                    nc.tensor.transpose(
+                        bank[:, (u * sub + s) * P : (u * sub + s + 1) * P],
+                        words[:, lo + u : lo + GROUP // 2 : 2],
+                        ident32[:],
+                    )
+            return bank
+
+        def inverse(bank, c, g):
+            sub = SUBS[c]
+            inv = work.tile([P, sub * P * PACK], F32, name="inv", tag="inv%d" % g, align_bytes=64)
+            turned = bank[:].bitcast(BF16).rearrange("p (u r e) -> p u r e", u=2, e=2)
+            for s0, s1, how in pieces(c, g):
+                dst = inv[:, s0 * P * PACK : s1 * P * PACK]
+                src = turned[:, :, s0 * P : s1 * P, :]
+                if how == "s":
+                    dst = dst.rearrange("p (u e r) -> p u e r", u=2, e=2)
+                    src = src.rearrange("p u r e -> p u e r")
+                else:
+                    dst = dst.rearrange("p (r u e) -> p r u e", u=2, e=2)
+                    src = src.rearrange("p u r e -> p r u e")
+                nc.scalar.activation(out=dst, in_=src, func=ACT.Abs_reciprocal_sqrt, bias=soft[:], scale=-2.0)
+            return inv
+
+        def weigh(inv, a, c, g, s0, s1, how):
+            rows = (s1 - s0) * P
+            cols = slice(s0 * P * PACK, s1 * P * PACK)
+            a_view = a[:, cols].rearrange("p (r t) -> p r t", t=PACK)
+            if how == "s":
+                am = work.tile([P, rows * PACK], BF16, name="am", tag="am%d" % g, align_bytes=64)
+                for t in range(PACK):
+                    nc.scalar.activation(
+                        out=am[:, t * rows : (t + 1) * rows],
+                        in_=inv[:, s0 * P * PACK + t * rows : s0 * P * PACK + (t + 1) * rows],
+                        func=ACT.Copy,
+                        scale=mass32[:, g * PACK + t : g * PACK + t + 1],
+                    )
+                nc.gpsimd.tensor_scalar(
+                    out=a_view, in0=am[:].rearrange("p (t r) -> p r t", t=PACK), scalar1=1.0, scalar2=0.0, op0=ALU.mult, op1=ALU.add
+                )
+                return
+            inv_view = inv[:, cols].rearrange("p (r t) -> p r t", t=PACK)
+            m = (mass_sq if how == "g" or c == 0 else mass_ps)[:, g * PACK : (g + 1) * PACK].unsqueeze(1).to_broadcast([P, rows, PACK])
+            if how == "g":
+                nc.gpsimd.tensor_tensor(out=a_view, in0=inv_view, in1=m, op=ALU.mult)
+            else:
+                nc.vector.tensor_tensor(out=a_view, in0=inv_view, in1=m, op=ALU.mult)
+
+        def quantise(a, c, g):
+            rows = SUBS[c] * P
+            codes = work.tile([P, rows], U32, name="codes", tag="codes%d" % g, align_bytes=64)
+            scales = work.tile([P, rows], U8, name="scales", tag="scales%d" % g, align_bytes=64)
+            nc.vector.quantize_mx(out=codes[:].bitcast(FP8X4), scales=scales[:], in_=a[:])
+            return codes, scales
+
+        def light_pass(acc, quant, g, s, h, first):
+            codes, scales = quant[g]
+            nc.tensor.matmul_mx(
+                out=acc[:],
+                lhsT=codes[:, s * P : (s + 1) * P].bitcast(FP8X4),
+                lhsT_scale=scales[:, s * P : (s + 1) * P],
+                rhs=l_words[:, g - 1, 2 * h * HALF : 2 * (h + 1) * HALF].bitcast(FP4X4),
+                rhs_scale=l_scales[:, g - 1, h * HALF : (h + 1) * HALF],
+                start=first,
+                stop=False,
+            )
+
+        def heavy_pass(acc, quant, s, h):
+            codes, scales = quant[0]
+            nc.tensor.matmul_mx(
+                out=acc[:],
+                lhsT=codes[:, s * P : (s + 1) * P].bitcast(FP8X4),
+                lhsT_scale=scales[:, s * P : (s + 1) * P],
+                rhs=h_codes[:, h * HALF : (h + 1) * HALF].bitcast(FP8X4),
+                rhs_scale=h_scales[:, h * HALF : (h + 1) * HALF],
+                start=False,
+                stop=True,
+            )
+
+        res_tiles = {}
+
+        def drain(acc, c, s, h):
+            if h == 0:
+                res = work.tile([P, N], F32, name="res", tag="res%d" % s, align_bytes=64)
+                res_tiles[(c, s)] = res
+            res = res_tiles[(c, s)]
+            cols = slice(h * HALF, (h + 1) * HALF)
+            nc.vector.tensor_tensor(out=res[:, cols], in0=acc[:], in1=bg[:, cols], op=ALU.add)
+            if c == CHUNKS - 1:
+                nc.sync.dma_start(out=out_rows[c][:, s, cols], in_=res[:, cols])
+            elif h == HALVES - 1:
+                nc.sync.dma_start(out=out_rows[c][:, s, :], in_=res[:])
+
+        def interleave(q, eng):
+            step = N // 4
+            dst = h_group[:, q * step : (q + 1) * step, :].rearrange("p (c i) t -> p c t i", i=4)
+            src = h_raw[:, :, q * step : (q + 1) * step].rearrange("p t (c i) -> p c t i", i=4)
+            if eng == "v":
+                nc.vector.tensor_copy(out=dst, in_=src)
+            elif eng == "s":
+                nc.scalar.copy(out=dst, in_=src)
+            else:
+                nc.gpsimd.tensor_scalar(out=dst, in0=src, scalar1=1.0, scalar2=0.0, op0=ALU.mult, op1=ALU.add)
+
+        def quantise_heavy(h):
+            cols = slice(h * HALF, (h + 1) * HALF)
+            nc.vector.quantize_mx(
+                out=h_codes[:, cols].bitcast(FP8X4),
+                scales=h_scales[:, cols],
+                in_=h_group[:, cols, :].rearrange("p n t -> p (n t)"),
+            )
+
+        def mass_to_psum():
+            mt_bank = turn.tile([P, 2 * HALF], BF16, name="mt_bank", tag="turn")
+            nc.tensor.transpose(mt_bank[:, 0:P], mass_sq[:], ident16[:])
+            mass_t = keep.tile([P, P], BF16, name="mass_t", align_bytes=64)
+            nc.vector.tensor_copy(out=mass_t[:], in_=mt_bank[:, 0:P])
+            nc.tensor.transpose(mass_ps[:], mass_t[:], ident16[:])
+
+        def turn_and_invert(c):
+            banks = {g: transposes(c, g) for g in G_ORDER}
+            return {g: inverse(banks[g], c, g) for g in G_ORDER}
+
+        def product(c, g):
+            if (c, g) not in weighed:
+                a = work.tile([P, SUBS[c] * P * PACK], BF16, name="a", tag="a%d" % g, align_bytes=64)
+                weighed[(c, g)] = a
+            return weighed[(c, g)]
+
+        def weigh_off_vector(c):
+            for g in G_ORDER:
+                for s0, s1, how in pieces(c, g):
+                    if how != "v":
+                        weigh(invs[c][g], product(c, g), c, g, s0, s1, how)
+
+        def weigh_on_vector(c):
+            for g in G_ORDER:
+                for s0, s1, how in pieces(c, g):
+                    if how == "v":
+                        weigh(invs[c][g], product(c, g), c, g, s0, s1, how)
+
+        def quantise_chunk(c):
+            return {g: quantise(weighed[(c, g)], c, g) for g in Q_ORDER}
+
+        weighed = {}
+        accs = {}
+
+        def spots(c):
+            return [(s, h) for s in range(SUBS[c]) for h in range(HALVES)]
+
+        def light_passes(c, s, h):
+            accs[(c, s, h)] = sums.tile([P, HALF], F32, name="acc", tag="acc")
+            light_pass(accs[(c, s, h)], quants[c], 1, s, h, True)
+            light_pass(accs[(c, s, h)], quants[c], 2, s, h, False)
+
+        quants = {0: {}, 1: {}}
+        invs = {0: turn_and_invert(0)}
+        mass_to_psum()
+        weigh_on_vector(0)
+        for g in Q_ORDER:
+            quants[0][g] = quantise(weighed[(0, g)], 0, g)
+        invs[1] = turn_and_invert(1)
+        for s, h in spots(0):
+            light_passes(0, s, h)
+        bgt_bank = turn.tile([P, 2 * HALF], BF16, name="bgt_bank", tag="turn")
+        nc.tensor.transpose(bgt_bank[:, 0:P], bg_rows[:], ident16[:])
+        bg_t = keep.tile([P, 8], BF16, name="bg_t", align_bytes=64)
+        nc.scalar.copy(out=bg_t[:], in_=bgt_bank[:, 0:8])
+        bg_bank = turn.tile([P, 2 * HALF], BF16, name="bg_bank", tag="turn")
+        for j in range(8):
+            nc.tensor.transpose(bg_bank[:, j * P : (j + 1) * P], bg_t[:, j : j + 1].to_broadcast([P, P]), ident16[:])
+        nc.scalar.copy(out=bg[:], in_=bg_bank[:])
+        interleave(0, "g")
+        interleave(1, "g")
+        weigh_off_vector(1)
+        weigh_on_vector(1)
+        interleave(2, H_ENG[0])
+        interleave(3, H_ENG[1])
+        invs[2] = turn_and_invert(2)
+        for g in (1, 2):
+            quants[1][g] = quantise(weighed[(1, g)], 1, g)
+        quantise_heavy(0)
+        quants[1][0] = quantise(weighed[(1, 0)], 1, 0)
+        quantise_heavy(1)
+        weigh_off_vector(2)
+        early = spots(1)[:2]
+        for s, h in early:
+            light_passes(1, s, h)
+        for s, h in spots(0):
+            heavy_pass(accs[(0, s, h)], quants[0], s, h)
+
+        for c in range(1, CHUNKS):
+            if c + 2 < CHUNKS:
+                invs[c + 2] = turn_and_invert(c + 2)
+            for s, h in spots(c):
+                if not (c == 1 and (s, h) in early):
+                    light_passes(c, s, h)
+                heavy_pass(accs[(c, s, h)], quants[c], s, h)
+            if c == 1:
+                for s, h in spots(0):
+                    drain(accs[(0, s, h)], 0, s, h)
+            if c + 1 < CHUNKS:
+                weigh_on_vector(c + 1)
+            for s, h in spots(c):
+                drain(accs[(c, s, h)], c, s, h)
+            if c + 1 < CHUNKS:
+                quants[c + 1] = quantise_chunk(c + 1)
+            if c + 2 < CHUNKS:
+                weigh_off_vector(c + 2)

@@ -20,33 +20,44 @@ ALU = mybir.AluOpType
 SOFT2 = 0.125
 P = 128
 PACK = 4
-GROUP = 512
+GROUP = P * PACK
 GROUPS = K // GROUP
-SUBS = [1, 2, 2, 2, 2, 2, 2, 2, 1]
-STARTS = [P * sum(SUBS[:c]) for c in range(len(SUBS))]
-CHUNKS = len(SUBS)
+PAIRS = GROUP // 2
 HALF = 512
-LOADS = ["g0", "s", "b", "g1", "L", "h0", "h1"] + ["g%d" % c for c in range(2, CHUNKS)]
-H_ENG = "vs"
-G_ORDER = (0, 1, 2)
-Q_ORDER = (1, 2, 0)
 HALVES = N // HALF
+QUARTER = N // 4
+
+TILES = [1, 2, 2, 2, 2, 2, 2, 2, 1]
+STARTS = [P * sum(TILES[:c]) for c in range(len(TILES))]
+CHUNKS = len(TILES)
+LAST = CHUNKS - 1
+
+ALL_ON_VECTOR = ("VV", "VV", "VV")
+HEAVY_ON_GPSIMD = ("GG", "VV", "VV")
+HEAVY_FIRST = ("GG", "SV", "VV")
+BALANCED = ("GS", "SV", "VV")
+
+
+def workers(c):
+    if c < 2:
+        return ALL_ON_VECTOR
+    if c == 2:
+        return HEAVY_FIRST
+    return HEAVY_ON_GPSIMD if c == LAST else BALANCED
+
+
+def runs(c, g):
+    who = workers(c)[g][: TILES[c]]
+    if len(set(who)) == 1 and who[0] != "S":
+        return [(0, TILES[c], who[0])]
+    return [(s, s + 1, w) for s, w in enumerate(who)]
 
 
 def tile_shell_nbody_potential_s1_kernel(tc, gram, mass, heavy, light_words, light_scales, background, out):
     nc = tc.nc
-    gram_rows = [gram[a : a + P * s, :].rearrange("(p s) k -> p s k", s=s) for a, s in zip(STARTS, SUBS)]
-    out_rows = [out[a : a + P * s, :].rearrange("(p s) n -> p s n", s=s) for a, s in zip(STARTS, SUBS)]
-
-    def pieces(c, g):
-        sub = SUBS[c]
-        if c < 3:
-            return [(0, sub, "v")]
-        if g == 0:
-            return [(0, sub, "g")]
-        if g == 1 and sub == 2:
-            return [(0, 1, "s"), (1, 2, "v")]
-        return [(0, sub, "v")]
+    gram_rows = [gram[a : a + P * n, :].rearrange("(p s) k -> p s k", s=n) for a, n in zip(STARTS, TILES)]
+    out_rows = [out[a : a + P * n, :].rearrange("(p s) n -> p s n", s=n) for a, n in zip(STARTS, TILES)]
+    heavy_rows = heavy.rearrange("(p t) n -> p t n", t=PACK)
 
     with ExitStack() as ctx:
         keep = ctx.enter_context(tc.tile_pool(name="keep", bufs=1))
@@ -58,273 +69,311 @@ def tile_shell_nbody_potential_s1_kernel(tc, gram, mass, heavy, light_words, lig
 
         grams = []
         for c in range(CHUNKS):
-            g_sb = keep.tile([P, SUBS[c], K], BF16, name="gram%d" % c, align_bytes=64)
-            grams.append(g_sb)
-        mass_raw = keep.tile([P, GROUPS * PACK], BF16, name="mass_raw", align_bytes=64)
+            gram_sb = keep.tile([P, TILES[c], K], BF16, name="gram%d" % c, align_bytes=64)
+            grams.append(gram_sb)
+        mass_rows = keep.tile([P, GROUP], BF16, name="mass_rows", align_bytes=64)
+        mass_cols = keep.tile([P, P], BF16, name="mass_cols", align_bytes=64)
+        mass_cols32 = keep.tile([P, GROUPS * PACK], F32, name="mass_cols32", align_bytes=64)
+        mass_turned = keep.tile([P, P], BF16, name="mass_turned", align_bytes=64)
+        mass_ps = fixed.tile([P, P], BF16, name="mass_ps")
         bg_rows = keep.tile([P, P], BF16, name="bg_rows", align_bytes=64)
-        mass_sq = keep.tile([P, P], BF16, name="mass_sq", align_bytes=64)
+        bg_cols = keep.tile([P, N // P], BF16, name="bg_cols", align_bytes=64)
+        bg = keep.tile([P, N], BF16, name="bg", align_bytes=64)
         l_words = keep.tile([P, 2, 2 * N], U8, name="l_words", align_bytes=64)
         l_scales = keep.tile([P, 2, N], U8, name="l_scales", align_bytes=64)
         h_raw = keep.tile([P, PACK, N], BF16, name="h_raw", align_bytes=64)
+        h_grouped = keep.tile([P, N, PACK], BF16, name="h_grouped", align_bytes=64)
+        h_codes = keep.tile([P, N], U32, name="h_codes", align_bytes=64)
+        h_scales = keep.tile([P, N], U8, name="h_scales", align_bytes=64)
         ident32 = keep.tile([P, P], F32, name="ident32", align_bytes=64)
         ident16 = keep.tile([P, P], BF16, name="ident16", align_bytes=64)
         soft = keep.tile([P, 1], F32, name="soft", align_bytes=64)
         warm = keep.tile([P, 1], F32, name="warm", align_bytes=64)
 
         make_identity(nc, ident32[:])
+        nc.vector.memset(mass_rows[:], 0.0)
         nc.vector.memset(soft[:], 2.0 + SOFT2)
         nc.vector.memset(bg_rows[:], 0.0)
         nc.vector.memset(l_scales[:].rearrange("p g n -> p (g n)").bitcast(I32), 0)
-        nc.vector.memset(mass_sq[:], 0.0)
+        nc.vector.memset(mass_cols[:], 0.0)
+        nc.vector.tensor_copy(out=ident16[:], in_=ident32[:])
 
-        nc.scalar.dma_start(out=mass_raw[:].rearrange("p (g t) -> p g t", t=PACK), in_=mass.rearrange("(g p t) -> p g t", p=P, t=PACK))
-        heavy_rows = heavy.rearrange("(p j) n -> p j n", j=PACK)
-
-        def load(what):
-            if what[0] == "g":
-                c = int(what[1:])
-                nc.sync.dma_start(out=grams[c][:], in_=gram_rows[c])
-            elif what == "L":
-                nc.sync.dma_start(out=l_words[:].bitcast(I32), in_=light_words.rearrange("g p b -> p g b").bitcast(I32))
-            elif what == "b":
-                nc.sync.dma_start(out=bg_rows[0:8, :], in_=background.rearrange("(j c) -> j c", c=P))
-            elif what == "s":
-                for q in range(4):
-                    nc.sync.dma_start(
-                        out=l_scales[32 * q : 32 * q + 4, :, :].bitcast(I32),
-                        in_=light_scales[:, 4 * q : 4 * q + 4, :].rearrange("g q n -> q g n").bitcast(I32),
-                    )
-            else:
-                h = int(what[1:])
-                nc.sync.dma_start(out=h_raw[:, :, h * HALF : (h + 1) * HALF], in_=heavy_rows[:, :, h * HALF : (h + 1) * HALF])
-
-        for what in LOADS:
-            load(what)
+        nc.scalar.dma_start(out=mass_rows[0:GROUPS, :], in_=mass.rearrange("(g k) -> g k", k=GROUP))
         nc.scalar.activation(out=warm[:], in_=soft[:], func=ACT.Abs_reciprocal_sqrt)
 
-        nc.vector.tensor_copy(out=ident16[:], in_=ident32[:])
-        nc.vector.tensor_copy(out=mass_sq[:, 0 : GROUPS * PACK], in_=mass_raw[:])
-        mass32 = keep.tile([P, GROUPS * PACK], F32, name="mass32", align_bytes=64)
-        nc.vector.tensor_copy(out=mass32[:], in_=mass_raw[:])
+        nc.sync.dma_start(out=grams[0][:], in_=gram_rows[0])
+        nc.sync.dma_start(out=bg_rows[0 : N // P, :], in_=background.rearrange("(j c) -> j c", c=P))
+        for q in range(4):
+            nc.sync.dma_start(
+                out=l_scales[32 * q : 32 * q + 4, :, :].bitcast(I32),
+                in_=light_scales[:, 4 * q : 4 * q + 4, :].rearrange("g r n -> r g n").bitcast(I32),
+            )
+        nc.sync.dma_start(out=grams[1][:], in_=gram_rows[1])
+        nc.sync.dma_start(out=l_words[:].bitcast(I32), in_=light_words.rearrange("g p b -> p g b").bitcast(I32))
+        for h in range(HALVES):
+            cols = slice(h * HALF, (h + 1) * HALF)
+            nc.sync.dma_start(out=h_raw[:, :, cols], in_=heavy_rows[:, :, cols])
+        for c in range(2, CHUNKS):
+            nc.sync.dma_start(out=grams[c][:], in_=gram_rows[c])
 
-        h_group = keep.tile([P, N, PACK], BF16, name="h_group", align_bytes=64)
-        h_codes = keep.tile([P, N], U32, name="h_codes", align_bytes=64)
-        h_scales = keep.tile([P, N], U8, name="h_scales", align_bytes=64)
-        mass_ps = fixed.tile([P, P], BF16, name="mass_ps")
-        bg = keep.tile([P, N], BF16, name="bg", align_bytes=64)
-
-        def transposes(c, g):
-            sub = SUBS[c]
-            bank = turn.tile([P, 2 * sub * P], F32, name="bank", tag="turn")
+        def turn_gram(c, g):
+            n = TILES[c]
+            bank = turn.tile([P, 2 * n * P], F32, name="bank", tag="turn")
             words = grams[c][:].rearrange("p s k -> p (s k)").bitcast(F32)
             for u in range(2):
-                for s in range(sub):
-                    lo = s * (K // 2) + g * (GROUP // 2)
+                for s in range(n):
+                    first = s * (K // 2) + g * PAIRS
                     nc.tensor.transpose(
-                        bank[:, (u * sub + s) * P : (u * sub + s + 1) * P],
-                        words[:, lo + u : lo + GROUP // 2 : 2],
+                        bank[:, (u * n + s) * P : (u * n + s + 1) * P],
+                        words[:, first + u : first + PAIRS : 2],
                         ident32[:],
                     )
             return bank
 
-        def inverse(bank, c, g):
-            sub = SUBS[c]
-            inv = work.tile([P, sub * P * PACK], F32, name="inv", tag="inv%d" % g, align_bytes=64)
+        inverses = {}
+
+        def invert(bank, c, g):
+            rows = TILES[c] * P
+            inv = work.tile([P, rows * PACK], F32, name="inv", tag="inv%d" % g, align_bytes=64)
             turned = bank[:].bitcast(BF16).rearrange("p (u r e) -> p u r e", u=2, e=2)
-            for s0, s1, how in pieces(c, g):
-                dst = inv[:, s0 * P * PACK : s1 * P * PACK]
-                src = turned[:, :, s0 * P : s1 * P, :]
-                if how == "s":
+            pieces = runs(c, g)
+            if all(worker != "S" for first, end, worker in pieces):
+                pieces = [(0, TILES[c], "V")]
+            for first, end, worker in pieces:
+                dst = inv[:, first * GROUP : end * GROUP]
+                src = turned[:, :, first * P : end * P, :]
+                if worker == "S":
                     dst = dst.rearrange("p (u e r) -> p u e r", u=2, e=2)
                     src = src.rearrange("p u r e -> p u e r")
                 else:
                     dst = dst.rearrange("p (r u e) -> p r u e", u=2, e=2)
                     src = src.rearrange("p u r e -> p r u e")
                 nc.scalar.activation(out=dst, in_=src, func=ACT.Abs_reciprocal_sqrt, bias=soft[:], scale=-2.0)
-            return inv
+            inverses[(c, g)] = inv
 
-        def weigh(inv, a, c, g, s0, s1, how):
-            rows = (s1 - s0) * P
-            cols = slice(s0 * P * PACK, s1 * P * PACK)
-            a_view = a[:, cols].rearrange("p (r t) -> p r t", t=PACK)
-            if how == "s":
-                am = work.tile([P, rows * PACK], BF16, name="am", tag="am%d" % g, align_bytes=64)
-                for t in range(PACK):
-                    nc.scalar.activation(
-                        out=am[:, t * rows : (t + 1) * rows],
-                        in_=inv[:, s0 * P * PACK + t * rows : s0 * P * PACK + (t + 1) * rows],
-                        func=ACT.Copy,
-                        scale=mass32[:, g * PACK + t : g * PACK + t + 1],
-                    )
-                nc.gpsimd.tensor_scalar(
-                    out=a_view, in0=am[:].rearrange("p (t r) -> p r t", t=PACK), scalar1=1.0, scalar2=0.0, op0=ALU.mult, op1=ALU.add
-                )
-                return
-            inv_view = inv[:, cols].rearrange("p (r t) -> p r t", t=PACK)
-            m = (mass_sq if how == "g" or c == 0 else mass_ps)[:, g * PACK : (g + 1) * PACK].unsqueeze(1).to_broadcast([P, rows, PACK])
-            if how == "g":
-                nc.gpsimd.tensor_tensor(out=a_view, in0=inv_view, in1=m, op=ALU.mult)
-            else:
-                nc.vector.tensor_tensor(out=a_view, in0=inv_view, in1=m, op=ALU.mult)
+        def turn_and_invert(c):
+            banks = [turn_gram(c, g) for g in range(GROUPS)]
+            for g in range(GROUPS):
+                invert(banks[g], c, g)
 
-        def quantise(a, c, g):
-            rows = SUBS[c] * P
-            codes = work.tile([P, rows], U32, name="codes", tag="codes%d" % g, align_bytes=64)
-            scales = work.tile([P, rows], U8, name="scales", tag="scales%d" % g, align_bytes=64)
-            nc.vector.quantize_mx(out=codes[:].bitcast(FP8X4), scales=scales[:], in_=a[:])
-            return codes, scales
+        values = {}
 
-        def light_pass(acc, quant, g, s, h, first):
-            codes, scales = quant[g]
-            nc.tensor.matmul_mx(
-                out=acc[:],
-                lhsT=codes[:, s * P : (s + 1) * P].bitcast(FP8X4),
-                lhsT_scale=scales[:, s * P : (s + 1) * P],
-                rhs=l_words[:, g - 1, 2 * h * HALF : 2 * (h + 1) * HALF].bitcast(FP4X4),
-                rhs_scale=l_scales[:, g - 1, h * HALF : (h + 1) * HALF],
-                start=first,
-                stop=False,
+        def values_of(c, g):
+            if (c, 0) not in values:
+                width = TILES[c] * GROUP
+                heavy_a = work.tile([P, width], BF16, name="heavy_a", align_bytes=64)
+                light_a = work.tile([P, 2 * width], BF16, name="light_a", align_bytes=64)
+                values[(c, 0)] = heavy_a[:]
+                values[(c, 1)] = light_a[:, 0:width]
+                values[(c, 2)] = light_a[:, width : 2 * width]
+                values[(c, "light")] = light_a[:]
+            return values[(c, g)]
+
+        def multiply(engine, mass_tile, c, g, first, end):
+            rows = (end - first) * P
+            cols = slice(first * GROUP, end * GROUP)
+            engine.tensor_tensor(
+                out=values_of(c, g)[:, cols].rearrange("p (r t) -> p r t", t=PACK),
+                in0=inverses[(c, g)][:, cols].rearrange("p (r t) -> p r t", t=PACK),
+                in1=mass_tile[:, g * PACK : (g + 1) * PACK].unsqueeze(1).to_broadcast([P, rows, PACK]),
+                op=ALU.mult,
             )
 
-        def heavy_pass(acc, quant, s, h):
-            codes, scales = quant[0]
-            nc.tensor.matmul_mx(
-                out=acc[:],
-                lhsT=codes[:, s * P : (s + 1) * P].bitcast(FP8X4),
-                lhsT_scale=scales[:, s * P : (s + 1) * P],
-                rhs=h_codes[:, h * HALF : (h + 1) * HALF].bitcast(FP8X4),
-                rhs_scale=h_scales[:, h * HALF : (h + 1) * HALF],
-                start=False,
-                stop=True,
-            )
+        def weigh_on_vector(c, mass_tile):
+            for g in range(GROUPS):
+                for first, end, worker in runs(c, g):
+                    if worker == "V":
+                        multiply(nc.vector, mass_tile, c, g, first, end)
 
-        res_tiles = {}
+        def weigh_off_vector(c):
+            held = work.tile([P, GROUPS * PACK], BF16, name="held", align_bytes=64)
+            nc.vector.tensor_copy(out=held[:], in_=mass_cols[:, 0 : GROUPS * PACK])
+            scaled = {}
+            for g in range(GROUPS):
+                for first, end, worker in runs(c, g):
+                    if worker == "S":
+                        half = work.tile([P, GROUP], BF16, name="half", tag="half%d" % g, align_bytes=64)
+                        for t in range(PACK):
+                            nc.scalar.activation(
+                                out=half[:, t * P : (t + 1) * P],
+                                in_=inverses[(c, g)][:, first * GROUP + t * P : first * GROUP + (t + 1) * P],
+                                func=ACT.Copy,
+                                scale=mass_cols32[:, g * PACK + t : g * PACK + t + 1],
+                            )
+                        scaled[(g, first)] = half
+            for g in range(GROUPS):
+                for first, end, worker in runs(c, g):
+                    if worker == "G":
+                        multiply(nc.gpsimd, held, c, g, first, end)
+                    if worker == "S":
+                        nc.gpsimd.tensor_scalar(
+                            out=values_of(c, g)[:, first * GROUP : end * GROUP].rearrange("p (r t) -> p r t", t=PACK),
+                            in0=scaled[(g, first)][:].rearrange("p (t r) -> p r t", t=PACK),
+                            scalar1=1.0,
+                            scalar2=0.0,
+                            op0=ALU.mult,
+                            op1=ALU.add,
+                        )
 
-        def drain(acc, c, s, h):
-            if h == 0:
-                res = work.tile([P, N], F32, name="res", tag="res%d" % s, align_bytes=64)
-                res_tiles[(c, s)] = res
-            res = res_tiles[(c, s)]
-            cols = slice(h * HALF, (h + 1) * HALF)
-            nc.vector.tensor_tensor(out=res[:, cols], in0=acc[:], in1=bg[:, cols], op=ALU.add)
-            if c == CHUNKS - 1:
-                nc.sync.dma_start(out=out_rows[c][:, s, cols], in_=res[:, cols])
-            elif h == HALVES - 1:
-                nc.sync.dma_start(out=out_rows[c][:, s, :], in_=res[:])
+        codes = {}
+        scales = {}
 
-        def interleave(q, eng):
-            step = N // 4
-            dst = h_group[:, q * step : (q + 1) * step, :].rearrange("p (c i) t -> p c t i", i=4)
-            src = h_raw[:, :, q * step : (q + 1) * step].rearrange("p t (c i) -> p c t i", i=4)
-            if eng == "v":
-                nc.vector.tensor_copy(out=dst, in_=src)
-            elif eng == "s":
-                nc.scalar.copy(out=dst, in_=src)
+        def quantise_light(c):
+            words = work.tile([P, 2 * TILES[c] * P], U32, name="light_words_a", align_bytes=64)
+            plane = work.tile([P, 2 * TILES[c] * P], U8, name="light_plane_a", align_bytes=64)
+            nc.vector.quantize_mx(out=words[:].bitcast(FP8X4), scales=plane[:], in_=values[(c, "light")])
+            codes[(c, "light")], scales[(c, "light")] = words, plane
+
+        def quantise_heavy_rows(c):
+            words = work.tile([P, TILES[c] * P], U32, name="heavy_words_a", align_bytes=64)
+            plane = work.tile([P, TILES[c] * P], U8, name="heavy_plane_a", align_bytes=64)
+            nc.vector.quantize_mx(out=words[:].bitcast(FP8X4), scales=plane[:], in_=values[(c, 0)])
+            codes[(c, "heavy")], scales[(c, "heavy")] = words, plane
+
+        def interleave_heavy(engine, quarter):
+            cols = slice(quarter * QUARTER, (quarter + 1) * QUARTER)
+            dst = h_grouped[:, cols, :].rearrange("p (c i) t -> p c t i", i=4)
+            src = h_raw[:, :, cols].rearrange("p t (c i) -> p c t i", i=4)
+            if engine is nc.vector:
+                engine.tensor_copy(out=dst, in_=src)
             else:
-                nc.gpsimd.tensor_scalar(out=dst, in0=src, scalar1=1.0, scalar2=0.0, op0=ALU.mult, op1=ALU.add)
+                engine.tensor_scalar(out=dst, in0=src, scalar1=1.0, scalar2=0.0, op0=ALU.mult, op1=ALU.add)
 
         def quantise_heavy(h):
             cols = slice(h * HALF, (h + 1) * HALF)
             nc.vector.quantize_mx(
                 out=h_codes[:, cols].bitcast(FP8X4),
                 scales=h_scales[:, cols],
-                in_=h_group[:, cols, :].rearrange("p n t -> p (n t)"),
+                in_=h_grouped[:, cols, :].rearrange("p n t -> p (n t)"),
             )
 
-        def mass_to_psum():
-            mt_bank = turn.tile([P, 2 * HALF], BF16, name="mt_bank", tag="turn")
-            nc.tensor.transpose(mt_bank[:, 0:P], mass_sq[:], ident16[:])
-            mass_t = keep.tile([P, P], BF16, name="mass_t", align_bytes=64)
-            nc.vector.tensor_copy(out=mass_t[:], in_=mt_bank[:, 0:P])
-            nc.tensor.transpose(mass_ps[:], mass_t[:], ident16[:])
-
-        def turn_and_invert(c):
-            banks = {g: transposes(c, g) for g in G_ORDER}
-            return {g: inverse(banks[g], c, g) for g in G_ORDER}
-
-        def product(c, g):
-            if (c, g) not in weighed:
-                a = work.tile([P, SUBS[c] * P * PACK], BF16, name="a", tag="a%d" % g, align_bytes=64)
-                weighed[(c, g)] = a
-            return weighed[(c, g)]
-
-        def weigh_off_vector(c):
-            for g in G_ORDER:
-                for s0, s1, how in pieces(c, g):
-                    if how != "v":
-                        weigh(invs[c][g], product(c, g), c, g, s0, s1, how)
-
-        def weigh_on_vector(c):
-            for g in G_ORDER:
-                for s0, s1, how in pieces(c, g):
-                    if how == "v":
-                        weigh(invs[c][g], product(c, g), c, g, s0, s1, how)
-
-        def quantise_chunk(c):
-            return {g: quantise(weighed[(c, g)], c, g) for g in Q_ORDER}
-
-        weighed = {}
         accs = {}
 
         def spots(c):
-            return [(s, h) for s in range(SUBS[c]) for h in range(HALVES)]
+            return [(s, h) for s in range(TILES[c]) for h in range(HALVES)]
 
         def light_passes(c, s, h):
-            accs[(c, s, h)] = sums.tile([P, HALF], F32, name="acc", tag="acc")
-            light_pass(accs[(c, s, h)], quants[c], 1, s, h, True)
-            light_pass(accs[(c, s, h)], quants[c], 2, s, h, False)
+            acc = sums.tile([P, HALF], F32, name="acc")
+            accs[(c, s, h)] = acc
+            for light in range(2):
+                cols = slice((light * TILES[c] + s) * P, (light * TILES[c] + s + 1) * P)
+                nc.tensor.matmul_mx(
+                    out=acc[:],
+                    lhsT=codes[(c, "light")][:, cols].bitcast(FP8X4),
+                    lhsT_scale=scales[(c, "light")][:, cols],
+                    rhs=l_words[:, light, 2 * h * HALF : 2 * (h + 1) * HALF].bitcast(FP4X4),
+                    rhs_scale=l_scales[:, light, h * HALF : (h + 1) * HALF],
+                    start=(light == 0),
+                    stop=False,
+                )
 
-        quants = {0: {}, 1: {}}
-        invs = {0: turn_and_invert(0)}
-        mass_to_psum()
-        weigh_on_vector(0)
-        for g in Q_ORDER:
-            quants[0][g] = quantise(weighed[(0, g)], 0, g)
-        invs[1] = turn_and_invert(1)
+        def heavy_pass(c, s, h):
+            rows = slice(s * P, (s + 1) * P)
+            cols = slice(h * HALF, (h + 1) * HALF)
+            nc.tensor.matmul_mx(
+                out=accs[(c, s, h)][:],
+                lhsT=codes[(c, "heavy")][:, rows].bitcast(FP8X4),
+                lhsT_scale=scales[(c, "heavy")][:, rows],
+                rhs=h_codes[:, cols].bitcast(FP8X4),
+                rhs_scale=h_scales[:, cols],
+                start=False,
+                stop=True,
+            )
+
+        results = {}
+
+        def drain(c, s, h):
+            if h == 0:
+                result = work.tile([P, N], F32, name="result", tag="result%d" % s, align_bytes=64)
+                results[(c, s)] = result
+            result = results[(c, s)]
+            parts = 2 if c == LAST and h == HALVES - 1 else 1
+            width = HALF // parts
+            for part in range(parts):
+                inside = slice(part * width, (part + 1) * width)
+                cols = slice(h * HALF + part * width, h * HALF + (part + 1) * width)
+                nc.vector.tensor_tensor(out=result[:, cols], in0=accs[(c, s, h)][:, inside], in1=bg[:, cols], op=ALU.add)
+                if c == LAST:
+                    nc.sync.dma_start(out=out_rows[c][:, s, cols], in_=result[:, cols])
+            if c < LAST and h == HALVES - 1:
+                nc.sync.dma_start(out=out_rows[c][:, s, :], in_=result[:])
+
+        banks = [turn_gram(0, 0)]
+        vectors = turn.tile([P, 2 * HALF], BF16, name="vectors", tag="turn")
+        for t in range(PACK):
+            nc.tensor.transpose(vectors[:, t * P : (t + 1) * P], mass_rows[:, t:GROUP:PACK], ident16[:])
+        nc.tensor.transpose(vectors[:, PACK * P : (PACK + 1) * P], bg_rows[:], ident16[:])
+        nc.vector.tensor_copy(
+            out=mass_cols[:, 0 : GROUPS * PACK].rearrange("p (g t) -> p g t", t=PACK),
+            in_=vectors[:, 0:GROUP].rearrange("p (t c) -> p c t", t=PACK)[:, 0:GROUPS, :],
+        )
+        nc.vector.tensor_copy(out=mass_cols32[:], in_=mass_cols[:, 0 : GROUPS * PACK])
+        nc.vector.tensor_copy(out=bg_cols[:], in_=vectors[:, PACK * P : PACK * P + N // P])
+        banks += [turn_gram(0, g) for g in (1, 2)]
+        for g in range(GROUPS):
+            invert(banks[g], 0, g)
+
+        multiply(nc.vector, mass_cols, 0, 0, 0, TILES[0])
+        mass_bank = turn.tile([P, P], BF16, name="mass_bank", tag="turn")
+        nc.tensor.transpose(mass_bank[:], mass_cols[:], ident16[:])
+        nc.vector.tensor_copy(out=mass_turned[:], in_=mass_bank[:])
+        for g in (1, 2):
+            multiply(nc.vector, mass_cols, 0, g, 0, TILES[0])
+        quantise_light(0)
+        quantise_heavy_rows(0)
+
+        banks = [turn_gram(1, 0)]
+        nc.tensor.transpose(mass_ps[:], mass_turned[:], ident16[:])
+        banks += [turn_gram(1, g) for g in (1, 2)]
+        for g in range(GROUPS):
+            invert(banks[g], 1, g)
         for s, h in spots(0):
             light_passes(0, s, h)
-        bgt_bank = turn.tile([P, 2 * HALF], BF16, name="bgt_bank", tag="turn")
-        nc.tensor.transpose(bgt_bank[:, 0:P], bg_rows[:], ident16[:])
-        bg_t = keep.tile([P, 8], BF16, name="bg_t", align_bytes=64)
-        nc.scalar.copy(out=bg_t[:], in_=bgt_bank[:, 0:8])
-        bg_bank = turn.tile([P, 2 * HALF], BF16, name="bg_bank", tag="turn")
-        for j in range(8):
-            nc.tensor.transpose(bg_bank[:, j * P : (j + 1) * P], bg_t[:, j : j + 1].to_broadcast([P, P]), ident16[:])
+
+        for quarter in (0, 1):
+            interleave_heavy(nc.gpsimd, quarter)
+        weigh_on_vector(1, mass_ps)
+        for quarter in (2, 3):
+            interleave_heavy(nc.vector, quarter)
+
+        for g in (0, 1):
+            invert(turn_gram(2, g), 2, g)
+        bg_bank = turn.tile([P, N], BF16, name="bg_bank", tag="turn")
+        for j in range(N // P):
+            nc.tensor.transpose(bg_bank[:, j * P : (j + 1) * P], bg_cols[:, j : j + 1].to_broadcast([P, P]), ident16[:])
         nc.scalar.copy(out=bg[:], in_=bg_bank[:])
-        interleave(0, "g")
-        interleave(1, "g")
-        weigh_off_vector(1)
-        weigh_on_vector(1)
-        interleave(2, H_ENG[0])
-        interleave(3, H_ENG[1])
-        invs[2] = turn_and_invert(2)
-        for g in (1, 2):
-            quants[1][g] = quantise(weighed[(1, g)], 1, g)
+        invert(turn_gram(2, 2), 2, 2)
+
+        quantise_light(1)
         quantise_heavy(0)
-        quants[1][0] = quantise(weighed[(1, 0)], 1, 0)
+        quantise_heavy_rows(1)
         quantise_heavy(1)
         weigh_off_vector(2)
-        early = spots(1)[:2]
+        early = spots(1)[:HALVES]
         for s, h in early:
             light_passes(1, s, h)
         for s, h in spots(0):
-            heavy_pass(accs[(0, s, h)], quants[0], s, h)
+            heavy_pass(0, s, h)
 
         for c in range(1, CHUNKS):
             if c + 2 < CHUNKS:
-                invs[c + 2] = turn_and_invert(c + 2)
+                turn_and_invert(c + 2)
             for s, h in spots(c):
-                if not (c == 1 and (s, h) in early):
+                if c > 1 or (s, h) not in early:
                     light_passes(c, s, h)
-                heavy_pass(accs[(c, s, h)], quants[c], s, h)
+                heavy_pass(c, s, h)
             if c == 1:
                 for s, h in spots(0):
-                    drain(accs[(0, s, h)], 0, s, h)
-            if c + 1 < CHUNKS:
-                weigh_on_vector(c + 1)
-            for s, h in spots(c):
-                drain(accs[(c, s, h)], c, s, h)
-            if c + 1 < CHUNKS:
-                quants[c + 1] = quantise_chunk(c + 1)
+                    drain(0, s, h)
+            if c < LAST:
+                weigh_on_vector(c + 1, mass_ps)
+            ahead = 2 if c == LAST - 1 else len(spots(c))
+            for s, h in spots(c)[:ahead]:
+                drain(c, s, h)
+            if c < LAST:
+                quantise_light(c + 1)
+                quantise_heavy_rows(c + 1)
+            for s, h in spots(c)[ahead:]:
+                drain(c, s, h)
             if c + 2 < CHUNKS:
                 weigh_off_vector(c + 2)

@@ -33,17 +33,17 @@ CHUNKS = len(TILES)
 LAST = CHUNKS - 1
 
 ALL_ON_VECTOR = ("VV", "VV", "VV")
-HEAVY_ON_GPSIMD = ("GG", "VV", "VV")
-HEAVY_FIRST = ("GG", "SV", "VV")
-BALANCED = ("GS", "SV", "VV")
+BALANCED = ("GG", "SV", "VV")
+LAST_SHARES = ("G", "V", "V")
+
+SORTED_FROM = 5
+SORTED_GROUP = 2
 
 
 def workers(c):
     if c < 2:
         return ALL_ON_VECTOR
-    if c == 2:
-        return HEAVY_FIRST
-    return HEAVY_ON_GPSIMD if c == LAST else BALANCED
+    return LAST_SHARES if c == LAST else BALANCED
 
 
 def runs(c, g):
@@ -120,14 +120,23 @@ def tile_shell_nbody_potential_s1_kernel(tc, gram, mass, heavy, light_words, lig
             n = TILES[c]
             bank = turn.tile([P, 2 * n * P], F32, name="bank", tag="turn")
             words = grams[c][:].rearrange("p s k -> p (s k)").bitcast(F32)
+            in_order = c >= SORTED_FROM and g == SORTED_GROUP
+            if in_order:
+                sorted_words = work.tile([P, n * PAIRS], F32, name="sorted_words", align_bytes=64)
+                nc.scalar.copy(
+                    out=sorted_words[:].rearrange("p (s u w) -> p s u w", s=n, u=2),
+                    in_=words.rearrange("p (s w) -> p s w", s=n)[:, :, g * PAIRS : (g + 1) * PAIRS].rearrange(
+                        "p s (w u) -> p s u w", u=2
+                    ),
+                )
             for u in range(2):
                 for s in range(n):
-                    first = s * (K // 2) + g * PAIRS
-                    nc.tensor.transpose(
-                        bank[:, (u * n + s) * P : (u * n + s + 1) * P],
-                        words[:, first + u : first + PAIRS : 2],
-                        ident32[:],
-                    )
+                    if in_order:
+                        source = sorted_words[:, s * PAIRS + u * P : s * PAIRS + (u + 1) * P]
+                    else:
+                        first = s * (K // 2) + g * PAIRS
+                        source = words[:, first + u : first + PAIRS : 2]
+                    nc.tensor.transpose(bank[:, (u * n + s) * P : (u * n + s + 1) * P], source, ident32[:])
             return bank
 
         inverses = {}
@@ -253,7 +262,7 @@ def tile_shell_nbody_potential_s1_kernel(tc, gram, mass, heavy, light_words, lig
             return [(s, h) for s in range(TILES[c]) for h in range(HALVES)]
 
         def light_passes(c, s, h):
-            acc = sums.tile([P, HALF], F32, name="acc")
+            acc = sums.tile([P, HALF], F32, name="acc", tag="acc")
             accs[(c, s, h)] = acc
             for light in range(2):
                 cols = slice((light * TILES[c] + s) * P, (light * TILES[c] + s + 1) * P)
@@ -327,8 +336,12 @@ def tile_shell_nbody_potential_s1_kernel(tc, gram, mass, heavy, light_words, lig
         banks += [turn_gram(1, g) for g in (1, 2)]
         for g in range(GROUPS):
             invert(banks[g], 1, g)
+        bg_bank = sums.tile([P, N], BF16, name="bg_bank", tag="acc")
         for s, h in spots(0):
             light_passes(0, s, h)
+        for j in range(N // P):
+            nc.tensor.transpose(bg_bank[:, j * P : (j + 1) * P], bg_cols[:, j : j + 1].to_broadcast([P, P]), ident16[:])
+        nc.scalar.copy(out=bg[:], in_=bg_bank[:])
 
         for quarter in (0, 1):
             interleave_heavy(nc.gpsimd, quarter)
@@ -336,13 +349,8 @@ def tile_shell_nbody_potential_s1_kernel(tc, gram, mass, heavy, light_words, lig
         for quarter in (2, 3):
             interleave_heavy(nc.vector, quarter)
 
-        for g in (0, 1):
+        for g in range(GROUPS):
             invert(turn_gram(2, g), 2, g)
-        bg_bank = turn.tile([P, N], BF16, name="bg_bank", tag="turn")
-        for j in range(N // P):
-            nc.tensor.transpose(bg_bank[:, j * P : (j + 1) * P], bg_cols[:, j : j + 1].to_broadcast([P, P]), ident16[:])
-        nc.scalar.copy(out=bg[:], in_=bg_bank[:])
-        invert(turn_gram(2, 2), 2, 2)
 
         quantise_light(1)
         quantise_heavy(0)

from contextlib import ExitStack

import concourse.mybir as mybir
from concourse.masks import make_identity

T, KH, KL, N = 2048, 512, 1024, 1024
K = KH + KL
FLOPS = 2 * T * K * N

F32 = mybir.dt.float32
BF16 = mybir.dt.bfloat16
I32 = mybir.dt.int32
U32 = mybir.dt.uint32
U8 = mybir.dt.uint8
FP8X4 = mybir.dt.float8_e4m3fn_x4
FP4X4 = mybir.dt.float4_e2m1fn_x4
ACT = mybir.ActivationFunctionType
ALU = mybir.AluOpType

SOFT2 = 0.125
P = 128
PACK = 4
GROUP = P * PACK
GROUPS = K // GROUP
PAIRS = GROUP // 2
HALF = 512
HALVES = N // HALF
QUARTER = N // 4

TILES = [1, 2, 2, 2, 2, 2, 2, 2, 1]
STARTS = [P * sum(TILES[:c]) for c in range(len(TILES))]
CHUNKS = len(TILES)
LAST = CHUNKS - 1

ALL_ON_VECTOR = ("VV", "VV", "VV")
BALANCED = ("GG", "SV", "VV")
LAST_SHARES = ("G", "V", "V")

SORTED_FROM = 5
SORTED_GROUP = 2


def workers(c):
    if c < 2:
        return ALL_ON_VECTOR
    return LAST_SHARES if c == LAST else BALANCED


def runs(c, g):
    who = workers(c)[g][: TILES[c]]
    if len(set(who)) == 1 and who[0] != "S":
        return [(0, TILES[c], who[0])]
    return [(s, s + 1, w) for s, w in enumerate(who)]


def tile_shell_nbody_potential_s1_kernel(tc, gram, mass, heavy, light_words, light_scales, background, out):
    nc = tc.nc
    gram_rows = [gram[a : a + P * n, :].rearrange("(p s) k -> p s k", s=n) for a, n in zip(STARTS, TILES)]
    out_rows = [out[a : a + P * n, :].rearrange("(p s) n -> p s n", s=n) for a, n in zip(STARTS, TILES)]
    heavy_rows = heavy.rearrange("(p t) n -> p t n", t=PACK)

    with ExitStack() as ctx:
        keep = ctx.enter_context(tc.tile_pool(name="keep", bufs=1))
        work = ctx.enter_context(tc.tile_pool(name="work", bufs=3))
        turn = ctx.enter_context(tc.psum_pool(name="turn", bufs=3))
        fixed = ctx.enter_context(tc.psum_pool(name="fixed", bufs=1))
        sums = ctx.enter_context(tc.psum_pool(name="sums", bufs=4))
        ctx.enter_context(tc.manual_schedule())

        grams = []
        for c in range(CHUNKS):
            gram_sb = keep.tile([P, TILES[c], K], BF16, name="gram%d" % c, align_bytes=64)
            grams.append(gram_sb)
        mass_rows = keep.tile([P, GROUP], BF16, name="mass_rows", align_bytes=64)
        mass_cols = keep.tile([P, P], BF16, name="mass_cols", align_bytes=64)
        mass_cols32 = keep.tile([P, GROUPS * PACK], F32, name="mass_cols32", align_bytes=64)
        mass_turned = keep.tile([P, P], BF16, name="mass_turned", align_bytes=64)
        mass_ps = fixed.tile([P, P], BF16, name="mass_ps")
        bg_rows = keep.tile([P, P], BF16, name="bg_rows", align_bytes=64)
        bg_cols = keep.tile([P, N // P], BF16, name="bg_cols", align_bytes=64)
        bg = keep.tile([P, N], BF16, name="bg", align_bytes=64)
        l_words = keep.tile([P, 2, 2 * N], U8, name="l_words", align_bytes=64)
        l_scales = keep.tile([P, 2, N], U8, name="l_scales", align_bytes=64)
        h_raw = keep.tile([P, PACK, N], BF16, name="h_raw", align_bytes=64)
        h_grouped = keep.tile([P, N, PACK], BF16, name="h_grouped", align_bytes=64)
        h_codes = keep.tile([P, N], U32, name="h_codes", align_bytes=64)
        h_scales = keep.tile([P, N], U8, name="h_scales", align_bytes=64)
        ident32 = keep.tile([P, P], F32, name="ident32", align_bytes=64)
        ident16 = keep.tile([P, P], BF16, name="ident16", align_bytes=64)
        soft = keep.tile([P, 1], F32, name="soft", align_bytes=64)
        warm = keep.tile([P, 1], F32, name="warm", align_bytes=64)

        make_identity(nc, ident32[:])
        nc.vector.memset(mass_rows[:], 0.0)
        nc.vector.memset(soft[:], 2.0 + SOFT2)
        nc.vector.memset(bg_rows[:], 0.0)
        nc.vector.memset(l_scales[:].rearrange("p g n -> p (g n)").bitcast(I32), 0)
        nc.vector.memset(mass_cols[:], 0.0)
        nc.vector.tensor_copy(out=ident16[:], in_=ident32[:])

        nc.scalar.dma_start(out=mass_rows[0:GROUPS, :], in_=mass.rearrange("(g k) -> g k", k=GROUP))
        nc.scalar.activation(out=warm[:], in_=soft[:], func=ACT.Abs_reciprocal_sqrt)

        nc.sync.dma_start(out=grams[0][:], in_=gram_rows[0])
        nc.sync.dma_start(out=bg_rows[0 : N // P, :], in_=background.rearrange("(j c) -> j c", c=P))
        for q in range(4):
            nc.sync.dma_start(
                out=l_scales[32 * q : 32 * q + 4, :, :].bitcast(I32),
                in_=light_scales[:, 4 * q : 4 * q + 4, :].rearrange("g r n -> r g n").bitcast(I32),
            )
        nc.sync.dma_start(out=grams[1][:], in_=gram_rows[1])
        nc.sync.dma_start(out=l_words[:].bitcast(I32), in_=light_words.rearrange("g p b -> p g b").bitcast(I32))
        for h in range(HALVES):
            cols = slice(h * HALF, (h + 1) * HALF)
            nc.sync.dma_start(out=h_raw[:, :, cols], in_=heavy_rows[:, :, cols])
        for c in range(2, CHUNKS):
            nc.sync.dma_start(out=grams[c][:], in_=gram_rows[c])

        def turn_gram(c, g):
            n = TILES[c]
            bank = turn.tile([P, 2 * n * P], F32, name="bank", tag="turn")
            words = grams[c][:].rearrange("p s k -> p (s k)").bitcast(F32)
            in_order = c >= SORTED_FROM and g == SORTED_GROUP
            if in_order:
                sorted_words = work.tile([P, n * PAIRS], F32, name="sorted_words", align_bytes=64)
                nc.scalar.copy(
                    out=sorted_words[:].rearrange("p (s u w) -> p s u w", s=n, u=2),
                    in_=words.rearrange("p (s w) -> p s w", s=n)[:, :, g * PAIRS : (g + 1) * PAIRS].rearrange(
                        "p s (w u) -> p s u w", u=2
                    ),
                )
            for u in range(2):
                for s in range(n):
                    if in_order:
                        source = sorted_words[:, s * PAIRS + u * P : s * PAIRS + (u + 1) * P]
                    else:
                        first = s * (K // 2) + g * PAIRS
                        source = words[:, first + u : first + PAIRS : 2]
                    nc.tensor.transpose(bank[:, (u * n + s) * P : (u * n + s + 1) * P], source, ident32[:])
            return bank

        inverses = {}

        def invert(bank, c, g):
            rows = TILES[c] * P
            inv = work.tile([P, rows * PACK], F32, name="inv", tag="inv%d" % g, align_bytes=64)
            turned = bank[:].bitcast(BF16).rearrange("p (u r e) -> p u r e", u=2, e=2)
            pieces = runs(c, g)
            if all(worker != "S" for first, end, worker in pieces):
                pieces = [(0, TILES[c], "V")]
            for first, end, worker in pieces:
                dst = inv[:, first * GROUP : end * GROUP]
                src = turned[:, :, first * P : end * P, :]
                if worker == "S":
                    dst = dst.rearrange("p (u e r) -> p u e r", u=2, e=2)
                    src = src.rearrange("p u r e -> p u e r")
                else:
                    dst = dst.rearrange("p (r u e) -> p r u e", u=2, e=2)
                    src = src.rearrange("p u r e -> p r u e")
                nc.scalar.activation(out=dst, in_=src, func=ACT.Abs_reciprocal_sqrt, bias=soft[:], scale=-2.0)
            inverses[(c, g)] = inv

        def turn_and_invert(c):
            banks = [turn_gram(c, g) for g in range(GROUPS)]
            for g in range(GROUPS):
                invert(banks[g], c, g)

        values = {}

        def values_of(c, g):
            if (c, 0) not in values:
                width = TILES[c] * GROUP
                heavy_a = work.tile([P, width], BF16, name="heavy_a", align_bytes=64)
                light_a = work.tile([P, 2 * width], BF16, name="light_a", align_bytes=64)
                values[(c, 0)] = heavy_a[:]
                values[(c, 1)] = light_a[:, 0:width]
                values[(c, 2)] = light_a[:, width : 2 * width]
                values[(c, "light")] = light_a[:]
            return values[(c, g)]

        def multiply(engine, mass_tile, c, g, first, end):
            rows = (end - first) * P
            cols = slice(first * GROUP, end * GROUP)
            engine.tensor_tensor(
                out=values_of(c, g)[:, cols].rearrange("p (r t) -> p r t", t=PACK),
                in0=inverses[(c, g)][:, cols].rearrange("p (r t) -> p r t", t=PACK),
                in1=mass_tile[:, g * PACK : (g + 1) * PACK].unsqueeze(1).to_broadcast([P, rows, PACK]),
                op=ALU.mult,
            )

        def weigh_on_vector(c, mass_tile):
            for g in range(GROUPS):
                for first, end, worker in runs(c, g):
                    if worker == "V":
                        multiply(nc.vector, mass_tile, c, g, first, end)

        def weigh_off_vector(c):
            held = work.tile([P, GROUPS * PACK], BF16, name="held", align_bytes=64)
            nc.vector.tensor_copy(out=held[:], in_=mass_cols[:, 0 : GROUPS * PACK])
            scaled = {}
            for g in range(GROUPS):
                for first, end, worker in runs(c, g):
                    if worker == "S":
                        half = work.tile([P, GROUP], BF16, name="half", tag="half%d" % g, align_bytes=64)
                        for t in range(PACK):
                            nc.scalar.activation(
                                out=half[:, t * P : (t + 1) * P],
                                in_=inverses[(c, g)][:, first * GROUP + t * P : first * GROUP + (t + 1) * P],
                                func=ACT.Copy,
                                scale=mass_cols32[:, g * PACK + t : g * PACK + t + 1],
                            )
                        scaled[(g, first)] = half
            for g in range(GROUPS):
                for first, end, worker in runs(c, g):
                    if worker == "G":
                        multiply(nc.gpsimd, held, c, g, first, end)
                    if worker == "S":
                        nc.gpsimd.tensor_scalar(
                            out=values_of(c, g)[:, first * GROUP : end * GROUP].rearrange("p (r t) -> p r t", t=PACK),
                            in0=scaled[(g, first)][:].rearrange("p (t r) -> p r t", t=PACK),
                            scalar1=1.0,
                            scalar2=0.0,
                            op0=ALU.mult,
                            op1=ALU.add,
                        )

        codes = {}
        scales = {}

        def quantise_light(c):
            words = work.tile([P, 2 * TILES[c] * P], U32, name="light_words_a", align_bytes=64)
            plane = work.tile([P, 2 * TILES[c] * P], U8, name="light_plane_a", align_bytes=64)
            nc.vector.quantize_mx(out=words[:].bitcast(FP8X4), scales=plane[:], in_=values[(c, "light")])
            codes[(c, "light")], scales[(c, "light")] = words, plane

        def quantise_heavy_rows(c):
            words = work.tile([P, TILES[c] * P], U32, name="heavy_words_a", align_bytes=64)
            plane = work.tile([P, TILES[c] * P], U8, name="heavy_plane_a", align_bytes=64)
            nc.vector.quantize_mx(out=words[:].bitcast(FP8X4), scales=plane[:], in_=values[(c, 0)])
            codes[(c, "heavy")], scales[(c, "heavy")] = words, plane

        def interleave_heavy(engine, quarter):
            cols = slice(quarter * QUARTER, (quarter + 1) * QUARTER)
            dst = h_grouped[:, cols, :].rearrange("p (c i) t -> p c t i", i=4)
            src = h_raw[:, :, cols].rearrange("p t (c i) -> p c t i", i=4)
            if engine is nc.vector:
                engine.tensor_copy(out=dst, in_=src)
            else:
                engine.tensor_scalar(out=dst, in0=src, scalar1=1.0, scalar2=0.0, op0=ALU.mult, op1=ALU.add)

        def quantise_heavy(h):
            cols = slice(h * HALF, (h + 1) * HALF)
            nc.vector.quantize_mx(
                out=h_codes[:, cols].bitcast(FP8X4),
                scales=h_scales[:, cols],
                in_=h_grouped[:, cols, :].rearrange("p n t -> p (n t)"),
            )

        accs = {}

        def spots(c):
            return [(s, h) for s in range(TILES[c]) for h in range(HALVES)]

        def light_passes(c, s, h):
            acc = sums.tile([P, HALF], F32, name="acc", tag="acc")
            accs[(c, s, h)] = acc
            for light in range(2):
                cols = slice((light * TILES[c] + s) * P, (light * TILES[c] + s + 1) * P)
                nc.tensor.matmul_mx(
                    out=acc[:],
                    lhsT=codes[(c, "light")][:, cols].bitcast(FP8X4),
                    lhsT_scale=scales[(c, "light")][:, cols],
                    rhs=l_words[:, light, 2 * h * HALF : 2 * (h + 1) * HALF].bitcast(FP4X4),
                    rhs_scale=l_scales[:, light, h * HALF : (h + 1) * HALF],
                    start=(light == 0),
                    stop=False,
                )

        def heavy_pass(c, s, h):
            rows = slice(s * P, (s + 1) * P)
            cols = slice(h * HALF, (h + 1) * HALF)
            nc.tensor.matmul_mx(
                out=accs[(c, s, h)][:],
                lhsT=codes[(c, "heavy")][:, rows].bitcast(FP8X4),
                lhsT_scale=scales[(c, "heavy")][:, rows],
                rhs=h_codes[:, cols].bitcast(FP8X4),
                rhs_scale=h_scales[:, cols],
                start=False,
                stop=True,
            )

        results = {}

        def drain(c, s, h):
            if h == 0:
                result = work.tile([P, N], F32, name="result", tag="result%d" % s, align_bytes=64)
                results[(c, s)] = result
            result = results[(c, s)]
            parts = 2 if c == LAST and h == HALVES - 1 else 1
            width = HALF // parts
            for part in range(parts):
                inside = slice(part * width, (part + 1) * width)
                cols = slice(h * HALF + part * width, h * HALF + (part + 1) * width)
                nc.vector.tensor_tensor(out=result[:, cols], in0=accs[(c, s, h)][:, inside], in1=bg[:, cols], op=ALU.add)
                if c == LAST:
                    nc.sync.dma_start(out=out_rows[c][:, s, cols], in_=result[:, cols])
            if c < LAST and h == HALVES - 1:
                nc.sync.dma_start(out=out_rows[c][:, s, :], in_=result[:])

        banks = [turn_gram(0, 0)]
        vectors = turn.tile([P, 2 * HALF], BF16, name="vectors", tag="turn")
        for t in range(PACK):
            nc.tensor.transpose(vectors[:, t * P : (t + 1) * P], mass_rows[:, t:GROUP:PACK], ident16[:])
        nc.tensor.transpose(vectors[:, PACK * P : (PACK + 1) * P], bg_rows[:], ident16[:])
        nc.vector.tensor_copy(
            out=mass_cols[:, 0 : GROUPS * PACK].rearrange("p (g t) -> p g t", t=PACK),
            in_=vectors[:, 0:GROUP].rearrange("p (t c) -> p c t", t=PACK)[:, 0:GROUPS, :],
        )
        nc.vector.tensor_copy(out=mass_cols32[:], in_=mass_cols[:, 0 : GROUPS * PACK])
        nc.vector.tensor_copy(out=bg_cols[:], in_=vectors[:, PACK * P : PACK * P + N // P])
        banks += [turn_gram(0, g) for g in (1, 2)]
        for g in range(GROUPS):
            invert(banks[g], 0, g)

        multiply(nc.vector, mass_cols, 0, 0, 0, TILES[0])
        mass_bank = turn.tile([P, P], BF16, name="mass_bank", tag="turn")
        nc.tensor.transpose(mass_bank[:], mass_cols[:], ident16[:])
        nc.vector.tensor_copy(out=mass_turned[:], in_=mass_bank[:])
        for g in (1, 2):
            multiply(nc.vector, mass_cols, 0, g, 0, TILES[0])
        quantise_light(0)
        quantise_heavy_rows(0)

        banks = [turn_gram(1, 0)]
        nc.tensor.transpose(mass_ps[:], mass_turned[:], ident16[:])
        banks += [turn_gram(1, g) for g in (1, 2)]
        for g in range(GROUPS):
            invert(banks[g], 1, g)
        bg_bank = sums.tile([P, N], BF16, name="bg_bank", tag="acc")
        for s, h in spots(0):
            light_passes(0, s, h)
        for j in range(N // P):
            nc.tensor.transpose(bg_bank[:, j * P : (j + 1) * P], bg_cols[:, j : j + 1].to_broadcast([P, P]), ident16[:])
        nc.scalar.copy(out=bg[:], in_=bg_bank[:])

        for quarter in (0, 1):
            interleave_heavy(nc.gpsimd, quarter)
        weigh_on_vector(1, mass_ps)
        for quarter in (2, 3):
            interleave_heavy(nc.vector, quarter)

        for g in range(GROUPS):
            invert(turn_gram(2, g), 2, g)

        quantise_light(1)
        quantise_heavy(0)
        quantise_heavy_rows(1)
        quantise_heavy(1)
        weigh_off_vector(2)
        early = spots(1)[:HALVES]
        for s, h in early:
            light_passes(1, s, h)
        for s, h in spots(0):
            heavy_pass(0, s, h)

        for c in range(1, CHUNKS):
            if c + 2 < CHUNKS:
                turn_and_invert(c + 2)
            for s, h in spots(c):
                if c > 1 or (s, h) not in early:
                    light_passes(c, s, h)
                heavy_pass(c, s, h)
            if c == 1:
                for s, h in spots(0):
                    drain(0, s, h)
            if c < LAST:
                weigh_on_vector(c + 1, mass_ps)
            ahead = 2 if c == LAST - 1 else len(spots(c))
            for s, h in spots(c)[:ahead]:
                drain(c, s, h)
            if c < LAST:
                quantise_light(c + 1)
                quantise_heavy_rows(c + 1)
            for s, h in spots(c)[ahead:]:
                drain(c, s, h)
            if c + 2 < CHUNKS:
                weigh_off_vector(c + 2)
